import numpy as np
import ml_dtypes


def mxq(x, axis, fmt="e4m3"):
    dtype, down = {"e4m3": (ml_dtypes.float8_e4m3fn, 7), "e5m2": (ml_dtypes.float8_e5m2, 14)}[fmt]
    v = np.moveaxis(np.asarray(x, np.float32).astype(ml_dtypes.bfloat16).astype(np.float64), axis, -1)
    blocks = v.reshape(v.shape[:-1] + (-1, 32))
    amax = np.abs(blocks).max(-1, keepdims=True)
    byte = np.maximum(np.where(amax > 0, np.frexp(amax)[1] - 1 + 127, 0) - down, 1)
    scale = np.exp2(byte - 127.0)
    codes = (blocks / scale).astype(np.float32).astype(dtype).astype(np.float64)
    return np.moveaxis((codes * scale).reshape(v.shape), -1, axis)


WIDE = False


def mx_kscale(k):
    if not WIDE:
        return np.ones(k)
    levels = np.array([10, -10, 5, -5, 0])
    if k % 512:
        return np.exp2(np.random.permutation(np.resize(levels, k // 32))).repeat(32)
    a = np.empty((k // 512, 16))
    for p in range(k // 512):
        a[p, :8] = np.random.permutation(np.resize(levels, 8))
        for g in range(8):
            far = levels[np.abs(levels - a[p, g]) >= 10]
            a[p, g + 8] = far[np.random.randint(len(far))]
    return np.exp2(a.ravel()).repeat(32)


def f64(x):
    return np.asarray(x).astype(np.float64)


def striped(idx):
    return np.tile(idx.reshape(-1, 16).T, (8, 1)).astype(np.uint16)


def unstriped(offs):
    return offs[:16].T.reshape(-1).astype(np.int64)


E2M1 = np.array([0.0, 0.5, 1.0, 1.5, 2.0, 3.0, 4.0, 6.0, -0.0, -0.5, -1.0, -1.5, -2.0, -3.0, -4.0, -6.0])


def pack_weight(w, fmt):
    k, n = w.shape
    w = f64(np.asarray(w, np.float32).astype(ml_dtypes.bfloat16)).reshape(k // 32, 32, n)
    amax = np.abs(w).max(1)
    if fmt == "e4m3":
        byte = np.frexp(amax)[1] - 1 + 127 - 7
    else:
        mant, ex = np.frexp(amax / 6.0)
        byte = np.where(mant > 0.5, ex, ex - 1) + 127
    byte = np.clip(np.where(amax > 0, byte, 1), 1, 254)
    scaled = (w * np.exp2(127.0 - byte)[:, None, :]).reshape(k, n).astype(np.float32)
    by_word = np.ascontiguousarray(scaled.reshape(k // 512, 128, 4, n).transpose(0, 1, 3, 2))
    if fmt == "e4m3":
        words = by_word.astype(ml_dtypes.float8_e4m3fn).view(np.uint8)
    else:
        c = by_word.astype(ml_dtypes.float4_e2m1fn).view(np.uint8) & 0xF
        words = (c[..., 0::2] | (c[..., 1::2] << 4)).reshape(k // 512, 128, 2 * n)
    return np.ascontiguousarray(words), np.ascontiguousarray(byte.astype(np.uint8).reshape(k // 512, 16, n))


def unpack_weight(words, scales, fmt):
    g, _, n = scales.shape
    words = np.ascontiguousarray(words).reshape(g, 128, n, -1)
    if fmt == "e4m3":
        vals = words.view(ml_dtypes.float8_e4m3fn).astype(np.float64)
    else:
        nib = np.empty((g, 128, n, 4), np.uint8)
        nib[..., 0::2] = words & 0xF
        nib[..., 1::2] = words >> 4
        vals = E2M1[nib]
    vals = vals * np.repeat(np.exp2(scales.astype(np.float64) - 127.0), 8, axis=1)[..., None]
    return vals.transpose(0, 1, 3, 2).reshape(g * 512, n)


def gelu(v):
    return 0.5 * v * (1.0 + np.tanh(np.sqrt(2.0 / np.pi) * (v + 0.044715 * v**3)))


K, H, T, S, P = 1024, 1024, 4096, 1024, 512


def setup_inputs():
    n = np.random.standard_normal
    s = mx_kscale(K)[:, None]
    u = mx_kscale(H)[:, None]
    tab_words, tab_scales = pack_weight(n((K, T)) * s, "e4m3")
    w1 = 1.2 * n((K, H)) / np.sqrt(K) / s
    gain = np.exp(0.3 * n(H)) * u[:, 0]
    w2 = 0.8 * n((H, H)) / np.sqrt(H) / u
    w3_words, w3_scales = pack_weight(0.4 * n((H, H)) / np.sqrt(H) / u, "e2m1")
    phase = np.random.uniform(-1.5, 1.5, H)
    skip = 0.6 * np.exp(0.3 * n(H)) / u[:, 0]
    wgo = np.exp(0.3 * n((128, P)))
    return {"tab_words": tab_words, "tab_scales": tab_scales,
            "offs": striped(np.random.permutation(T)[:S]),
            "pos1": striped(np.random.permutation(S)[:P]),
            "w1": w1.astype(np.float32), "gain": gain.astype(np.float32),
            "w2": w2.astype(np.float32),
            "w3_words": w3_words, "w3_scales": w3_scales,
            "phase": phase.astype(np.float32), "skip": skip.astype(np.float32),
            "wgo": wgo.astype(np.float32)}


def reference(tab_words, tab_scales, offs, pos1, w1, gain, w2, w3_words, w3_scales, phase, skip, wgo):
    v = unpack_weight(tab_words, tab_scales, "e4m3")[:, unstriped(offs)]
    h = f64(gain)[:, None] * np.tanh(mxq(f64(w1), 0, "e4m3").T @ v)
    x = mxq(h[:, unstriped(pos1)], 0, "e4m3")
    lin = mxq(f64(w2), 0, "e4m3").T @ x
    w3 = unpack_weight(w3_words, w3_scales, "e2m1")
    wave = np.sin((w3.T @ x) + f64(phase)[:, None])
    y = np.maximum(lin, wave)
    out = f64(skip)[:, None] * h
    out[:, unstriped(pos1)] = np.tile(f64(wgo), (H // 128, 1)) * y
    return out

@@ -1,0 +1,322 @@
+import math
+from contextlib import ExitStack
+
+import concourse.mybir as mybir
+
+K, H, T, S, M = 1024, 1024, 4096, 1024, 512
+FLOPS = 2 * K * H * S + 2 * 2 * H * H * M
+
+F32 = mybir.dt.float32
+BF16 = mybir.dt.bfloat16
+I32 = mybir.dt.int32
+U32 = mybir.dt.uint32
+U16 = mybir.dt.uint16
+U8 = mybir.dt.uint8
+FP8X4 = mybir.dt.float8_e4m3fn_x4
+FP4X4 = mybir.dt.float4_e2m1fn_x4
+ALU = mybir.AluOpType
+ACT = mybir.ActivationFunctionType
+
+P = 128
+PACK = 4
+PASS = P * PACK
+BANK = 512
+ROUNDER = 1.5 * 2.0**23
+TURN = 2.0 * math.pi
+KB = 1024
+
+
+def tile_list_press_ghosting_features_kernel(
+    tc, tab_words, tab_scales, offs, pos1, w1, gain, w2, w3_words, w3_scales, phase, skip, wgo, out
+):
+    nc = tc.nc
+    with ExitStack() as ctx:
+        keep = ctx.enter_context(tc.tile_pool(name="keep", bufs=1))
+        laid = ctx.enter_context(tc.tile_pool(name="laid", bufs=1))
+        ring = ctx.enter_context(tc.tile_pool(name="ring", bufs=2))
+        psum = ctx.enter_context(tc.psum_pool(name="psum", bufs=8))
+
+        def place(name, shape, dtype, kb):
+            return laid.tile(shape, dtype, name=name, offset=kb * KB, align_bytes=64)
+
+        TAB1, XG, PICK, TANH, PAGE, TAB0 = 10, 26, 32, 48, 80, 96
+
+        offs_sb = keep.tile([P, S // 16], U16, name="offs_sb")
+        pos_sb = keep.tile([P, M // 16], U16, name="pos_sb")
+        nc.sync.dma_start(offs_sb[:], offs)
+        w3_raw = keep.tile([P, 2, H // 2], I32, name="w3_raw", align_bytes=64)
+        nc.sync.dma_start(w3_raw[:], w3_words.bitcast(I32).rearrange("a p c -> p a c"))
+
+        tab_sc = place("tab_sc", [P, T // 4], I32, 0)
+        w3_sc_raw = place("w3_sc_raw", [P, 2, H // 4], I32, 4)
+        nc.vector.memset(tab_sc[:], 0)
+        nc.vector.memset(w3_sc_raw[:], 0)
+        for q in range(4):
+            nc.gpsimd.dma_start(tab_sc[32 * q : 32 * q + 8, :], tab_scales.bitcast(I32)[:, 4 * q : 4 * q + 4, :])
+        for q in range(4):
+            nc.gpsimd.dma_start(
+                w3_sc_raw[32 * q : 32 * q + 4, :, :],
+                w3_scales.bitcast(I32)[:, 4 * q : 4 * q + 4, :].rearrange("a r c -> r a c"),
+            )
+        gain_sb = keep.tile([P, 2, PACK], F32, name="gain_sb")
+        skip_sb = keep.tile([P, 2, PACK], F32, name="skip_sb")
+        phase_sb = keep.tile([P, 2, PACK], F32, name="phase_sb")
+        skip_gain = keep.tile([P, 2, PACK], F32, name="skip_gain")
+        phase_turns = keep.tile([P, 2, PACK], F32, name="phase_turns")
+
+        tab = [place("tab0", [P, T], I32, TAB0), place("tab1", [P, T], I32, TAB1)]
+
+        def load_tab(a):
+            nc.sync.dma_start(tab[a][:], tab_words[a].rearrange("p t i -> p (t i)").bitcast(I32))
+
+        raw = {}
+
+        def load_w(name, w, a, b):
+            t = ring.tile([P, PACK, PASS], F32, name="raw", tag="raw", bufs=6, align_bytes=64)
+            nc.sync.dma_start(
+                t[:], w[a * PASS : (a + 1) * PASS, b * PASS : (b + 1) * PASS].rearrange("(p j) c -> p j c", j=PACK)
+            )
+            raw[name, a, b] = t
+
+        load_tab(0)
+        load_w("w1", w1, 0, 0)
+        load_tab(1)
+        load_w("w1", w1, 1, 0)
+        nc.sync.dma_start(pos_sb[:], pos1)
+        load_w("w1", w1, 0, 1)
+        for dst, src in ((gain_sb, gain), (skip_sb, skip), (phase_sb, phase)):
+            nc.sync.dma_start(dst[:], src.rearrange("(b p t) -> p b t", b=2, t=PACK))
+        load_w("w1", w1, 1, 1)
+        load_w("w2", w2, 0, 0)
+        load_w("w2", w2, 1, 0)
+        wgo_sb = keep.tile([P, PACK, M], F32, name="wgo_sb")
+        for q in (0, 2, 1, 3):
+            nc.sync.dma_start(wgo_sb[32 * q : 32 * q + 32], wgo.rearrange("(r t) m -> r t m", t=PACK))
+        nc.gpsimd.tensor_tensor(skip_gain[:], skip_sb[:], gain_sb[:], ALU.mult)
+        nc.gpsimd.tensor_scalar(phase_turns[:], phase_sb[:], 1.0 / TURN, 0.0, ALU.mult, ALU.add)
+
+        w3_w = keep.tile([P, 2, H], U16, name="w3_w", align_bytes=64)
+        w3_s = keep.tile([P, 2, H], U8, name="w3_s", align_bytes=64)
+        nc.vector.tensor_copy(
+            w3_w[:].rearrange("p a (b t m) -> p (a b) t m", b=2, t=PACK),
+            w3_raw[:].bitcast(U16).rearrange("p a (b m t) -> p (a b) t m", b=2, t=PACK),
+        )
+
+        grouped, codes, scales = {}, {}, {}
+
+        def group(name, a, b, t0, t1, copy, kb):
+            g = place(f"g{name}_{a}{b}{t0}", [P, t1 - t0, P, PACK], BF16, kb)
+            src = raw[name, a, b][:].rearrange("p j (m t) -> p m t j", t=PACK)[:, :, t0:t1, :]
+            copy(g[:].rearrange("p t m j -> p m t j"), src)
+            grouped[name, a, b, t0] = g
+
+        def quantise(name, a, b, t0):
+            g = grouped[name, a, b, t0]
+            n = g.shape[1]
+            c = keep.tile([P, n * P], U32, name=f"c{name}_{a}{b}{t0}", align_bytes=64)
+            s = keep.tile([P, n * P], U8, name=f"s{name}_{a}{b}{t0}", align_bytes=64)
+            nc.vector.quantize_mx(out=c[:].bitcast(FP8X4), scales=s[:], in_=g[:].rearrange("p t m j -> p (t m j)"))
+            for t in range(n):
+                codes[name, a, b, t0 + t] = c[:, t * P : (t + 1) * P]
+                scales[name, a, b, t0 + t] = s[:, t * P : (t + 1) * P]
+
+        v_w, v_s = {}, {}
+
+        def gather_words(a, hf):
+            nc.vector.tensor_copy(
+                v_w[a][:, hf * BANK : (hf + 1) * BANK],
+                tab[a][:].bitcast(U32).indirect(offs_sb[:, 32 * hf : 32 * hf + 32]),
+            )
+
+        def gather_scales(hf):
+            t = keep.tile([P, BANK], U8, name=f"vs{hf}", align_bytes=64)
+            nc.vector.tensor_copy(t[:], tab_sc[:].bitcast(U8).indirect(offs_sb[:, 32 * hf : 32 * hf + 32]))
+            v_s[hf] = t
+
+        banks = {}
+
+        def mm1(b, t, hf, a):
+            if a == 0:
+                banks[b, t, hf] = psum.tile([P, BANK], F32, name="bank", tag="bank")
+            nc.tensor.matmul_mx(
+                out=banks[b, t, hf][:],
+                lhsT=codes["w1", a, b, t].bitcast(FP8X4),
+                lhsT_scale=scales["w1", a, b, t],
+                rhs=v_w[a][:, hf * BANK : (hf + 1) * BANK].bitcast(FP8X4),
+                rhs_scale=v_s[hf][4 * a : P, :],
+                start=(a == 0),
+                stop=(a == 1),
+            )
+
+        tanh_sb, picked, x_pairs = {}, {}, {}
+
+        def read_out(b, t):
+            th = place(f"tanh{b}{t}", [P, S], F32, TANH + 4 * (PACK * b + t))
+            for hf in range(2):
+                nc.scalar.activation(th[:, hf * BANK : (hf + 1) * BANK], banks[b, t, hf][:], ACT.Tanh)
+            tanh_sb[b, t] = th
+
+        def pick(b, t):
+            g = place(f"picked{b}{t}", [P, M], F32, PICK + 2 * (PACK * b + t))
+            nc.vector.tensor_copy(g[:], tanh_sb[b, t][:].indirect(pos_sb[:]))
+            picked[b, t] = g
+
+        def scale_round(b, t):
+            if t == 0:
+                x_pairs[b] = place(f"x_pairs{b}", [P, 2, M, 2], BF16, PAGE)
+            nc.scalar.activation(
+                x_pairs[b][:, t // 2, :, t % 2], picked[b, t][:], ACT.Copy, scale=gain_sb[:, b, t : t + 1]
+            )
+
+        def quantise_x(b):
+            g = place(f"xg{b}", [P, M, 2], I32, XG)
+            nc.vector.tensor_copy(g[:], x_pairs[b][:].rearrange("p u m e -> p u (m e)").bitcast(I32).rearrange("p u m -> p m u"))
+            c = keep.tile([P, M], U32, name=f"xc{b}", align_bytes=64)
+            s = keep.tile([P, M], U8, name=f"xs{b}", align_bytes=64)
+            nc.vector.quantize_mx(
+                out=c[:].bitcast(FP8X4), scales=s[:], in_=g[:].rearrange("p m u -> p (m u)").bitcast(BF16)
+            )
+            codes["x", b], scales["x", b] = c, s
+
+        slices = [(b, t) for b in range(2) for t in range(PACK)]
+        z_bank, lin, turns, frac = {}, {}, {}, {}
+
+        def mm_z(i, a):
+            b, t = slices[i]
+            if a == 0:
+                z_bank[i] = psum.tile([P, M], F32, name="z", tag="bank")
+            c0 = b * PASS + t * P
+            nc.tensor.matmul_mx(
+                out=z_bank[i][:],
+                lhsT=w3_w[:, a, c0 : c0 + P].bitcast(FP4X4),
+                lhsT_scale=w3_s[:, a, c0 : c0 + P],
+                rhs=codes["x", a][:].bitcast(FP8X4),
+                rhs_scale=scales["x", a][:],
+                start=(a == 0),
+                stop=(a == 1),
+            )
+
+        v_w[0] = keep.tile([P, S], U32, name="v0", align_bytes=64)
+        for hf in range(2):
+            gather_scales(hf)
+        for hf in range(2):
+            gather_words(0, hf)
+        group("w1", 0, 0, 0, PACK, nc.scalar.copy, 6)
+        quantise("w1", 0, 0, 0)
+        nc.vector.tensor_copy(
+            w3_s[:].rearrange("p a (b t m) -> p (a b) t m", b=2, t=PACK),
+            w3_sc_raw[:].bitcast(U8).rearrange("p a (b m t) -> p (a b) t m", b=2, t=PACK),
+        )
+        for t in range(PACK):
+            for hf in range(2):
+                mm1(0, t, hf, 0)
+        v_w[1] = place("v1", [P, S], U32, 3)
+        for hf in range(2):
+            gather_words(1, hf)
+        group("w1", 1, 0, 0, 2, nc.vector.tensor_copy, TAB1)
+        group("w1", 1, 0, 2, PACK, nc.scalar.copy, XG)
+        quantise("w1", 1, 0, 0)
+        quantise("w1", 1, 0, 2)
+        load_w("w2", w2, 0, 1)
+        load_w("w2", w2, 1, 1)
+
+        for t in range(PACK):
+            for hf in range(2):
+                mm1(0, t, hf, 1)
+            read_out(0, t)
+            if t in (0, 2):
+                group("w1", t // 2, 1, 0, PACK, nc.vector.tensor_copy, TAB1)
+                quantise("w1", t // 2, 1, 0)
+            pick(0, t)
+        for t in range(PACK):
+            scale_round(0, t)
+        for t in range(PACK):
+            for hf in range(2):
+                for a in range(2):
+                    mm1(1, t, hf, a)
+            read_out(1, t)
+            if t == 0:
+                quantise_x(0)
+            pick(1, t)
+            if t > 0:
+                scale_round(1, t - 1)
+        for i in range(2):
+            mm_z(i, 0)
+        scale_round(1, PACK - 1)
+        group("w2", 0, 0, 0, 2, nc.scalar.copy, PICK + 2 * (2 * PACK - 1))
+        quantise_x(1)
+        group("w2", 1, 0, 0, 2, nc.vector.tensor_copy, XG)
+        quantise("w2", 0, 0, 0)
+        quantise("w2", 1, 0, 0)
+        group("w2", 0, 0, 2, PACK, nc.vector.tensor_copy, XG + 2)
+        quantise("w2", 0, 0, 2)
+
+        page, y = {}, {}
+        last = len(slices) - 1
+
+        def to_turns(i):
+            b, t = slices[i]
+            if i >= 2:
+                mm_z(i, 0)
+            mm_z(i, 1)
+            turns[i] = ring.tile([P, M], F32, name="turns", tag="turns", bufs=4)
+            nc.scalar.activation(
+                turns[i][:], z_bank[i][:], ACT.Identity, bias=phase_turns[:, b, t : t + 1], scale=1.0 / TURN
+            )
+
+        def take_fraction(i):
+            whole = place(f"whole{i}", [P, M], U32, PAGE + 4 * i if i > 0 else PICK)
+            nc.scalar.activation(whole[:], turns[i][:], ACT.Copy, bias=ROUNDER)
+            frac[i] = ring.tile([P, M], F32, name="frac", tag="frac", bufs=3)
+            nc.vector.scalar_tensor_tensor(
+                frac[i][:], whole[:].bitcast(I32), ROUNDER, turns[i][:], ALU.subtract, ALU.subtract
+            )
+
+        def fill_page(i):
+            b, t = slices[i]
+            page[i] = place(f"page{i}", [P, S], F32, PAGE + 4 * i)
+            nc.scalar.activation(page[i][:], tanh_sb[b, t][:], ACT.Copy, scale=skip_gain[:, b, t : t + 1])
+
+        out_rows = out.rearrange("(b p t) j -> b t p j", b=2, t=PACK)
+
+        def larger(i):
+            b, t = slices[i]
+            ln = psum.tile([P, M], F32, name="lin", tag="bank")
+            for a in range(2):
+                nc.tensor.matmul_mx(
+                    out=ln[:],
+                    lhsT=codes["w2", a, b, t].bitcast(FP8X4),
+                    lhsT_scale=scales["w2", a, b, t],
+                    rhs=codes["x", a][:].bitcast(FP8X4),
+                    rhs_scale=scales["x", a][:],
+                    start=(a == 0),
+                    stop=(a == 1),
+                )
+            wave = ring.tile([P, M], F32, name="wave", tag="wave", bufs=3)
+            nc.scalar.activation(wave[:], frac[i][:], ACT.Sin, scale=-TURN)
+            y[i] = ring.tile([P, M], F32, name="y", tag="y", bufs=2)
+            nc.vector.tensor_tensor(y[i][:], ln[:], wave[:], ALU.max)
+
+        def put(i):
+            b, t = slices[i]
+            nc.vector.tensor_tensor(page[i][:].indirect(pos_sb[:]), y[i][:], wgo_sb[:, t, :], ALU.mult)
+            nc.sync.dma_start(out_rows[b, t], page[i][:])
+
+        later_groups = [(1, 0, 2), (0, 1, 0), (1, 1, 0), (0, 1, 2), (1, 1, 2)]
+        fill_page(0)
+        for i in range(2):
+            to_turns(i)
+            take_fraction(i)
+        for i in range(len(slices)):
+            if i + 2 <= last:
+                to_turns(i + 2)
+            larger(i)
+            if i + 2 <= last:
+                take_fraction(i + 2)
+            if i > 0:
+                fill_page(i)
+            put(i)
+            if i < len(later_groups):
+                a, b, t0 = later_groups[i]
+                group("w2", a, b, t0, t0 + 2, nc.scalar.copy, TANH + 4 * i)
+                quantise("w2", a, b, t0)

@@ -41,6 +41,10 @@ def tile_list_press_ghosting_features_kernel(
 
         TAB1, XG, PICK, TANH, PAGE, TAB0 = 10, 26, 32, 48, 80, 96
 
+        warm = keep.tile([P, 1], F32, name="warm")
+        warm_out = keep.tile([P, 1], F32, name="warm_out")
+        nc.gpsimd.memset(warm[:], 0.0)
+        nc.scalar.activation(warm_out[:], warm[:], ACT.Silu)
         offs_sb = keep.tile([P, S // 16], U16, name="offs_sb")
         pos_sb = keep.tile([P, M // 16], U16, name="pos_sb")
         nc.sync.dma_start(offs_sb[:], offs)
@@ -51,13 +55,6 @@ def tile_list_press_ghosting_features_kernel(
         w3_sc_raw = place("w3_sc_raw", [P, 2, H // 4], I32, 4)
         nc.vector.memset(tab_sc[:], 0)
         nc.vector.memset(w3_sc_raw[:], 0)
-        for q in range(4):
-            nc.gpsimd.dma_start(tab_sc[32 * q : 32 * q + 8, :], tab_scales.bitcast(I32)[:, 4 * q : 4 * q + 4, :])
-        for q in range(4):
-            nc.gpsimd.dma_start(
-                w3_sc_raw[32 * q : 32 * q + 4, :, :],
-                w3_scales.bitcast(I32)[:, 4 * q : 4 * q + 4, :].rearrange("a r c -> r a c"),
-            )
         gain_sb = keep.tile([P, 2, PACK], F32, name="gain_sb")
         skip_sb = keep.tile([P, 2, PACK], F32, name="skip_sb")
         phase_sb = keep.tile([P, 2, PACK], F32, name="phase_sb")
@@ -79,6 +76,13 @@ def tile_list_press_ghosting_features_kernel(
             raw[name, a, b] = t
 
         load_tab(0)
+        for q in range(4):
+            nc.sync.dma_start(tab_sc[32 * q : 32 * q + 8, :], tab_scales.bitcast(I32)[:, 4 * q : 4 * q + 4, :])
+        for q in range(4):
+            nc.sync.dma_start(
+                w3_sc_raw[32 * q : 32 * q + 4, :, :],
+                w3_scales.bitcast(I32)[:, 4 * q : 4 * q + 4, :].rearrange("a r c -> r a c"),
+            )
         load_w("w1", w1, 0, 0)
         load_tab(1)
         load_w("w1", w1, 1, 0)
@@ -161,12 +165,14 @@ def tile_list_press_ghosting_features_kernel(
             nc.vector.tensor_copy(g[:], tanh_sb[b, t][:].indirect(pos_sb[:]))
             picked[b, t] = g
 
-        def scale_round(b, t):
+        def scale_round(b, t, on_vector):
             if t == 0:
-                x_pairs[b] = place(f"x_pairs{b}", [P, 2, M, 2], BF16, PAGE)
-            nc.scalar.activation(
-                x_pairs[b][:, t // 2, :, t % 2], picked[b, t][:], ACT.Copy, scale=gain_sb[:, b, t : t + 1]
-            )
+                x_pairs[b] = place(f"x_pairs{b}", [P, 2, M, 2], BF16, PAGE + 4 * (1 - b))
+            dst = x_pairs[b][:, t // 2, :, t % 2]
+            if on_vector:
+                nc.vector.tensor_scalar(dst, picked[b, t][:], gain_sb[:, b, t : t + 1], None, ALU.mult)
+            else:
+                nc.scalar.activation(dst, picked[b, t][:], ACT.Copy, scale=gain_sb[:, b, t : t + 1])
 
         def quantise_x(b):
             g = place(f"xg{b}", [P, M, 2], I32, XG)
@@ -229,20 +235,19 @@ def tile_list_press_ghosting_features_kernel(
                 quantise("w1", t // 2, 1, 0)
             pick(0, t)
         for t in range(PACK):
-            scale_round(0, t)
-        for t in range(PACK):
             for hf in range(2):
                 for a in range(2):
                     mm1(1, t, hf, a)
             read_out(1, t)
-            if t == 0:
-                quantise_x(0)
+        for t in range(PACK):
+            scale_round(0, t, False)
+        for t in range(PACK):
             pick(1, t)
-            if t > 0:
-                scale_round(1, t - 1)
+            if t == 1:
+                quantise_x(0)
+            scale_round(1, t, t >= 2)
         for i in range(2):
             mm_z(i, 0)
-        scale_round(1, PACK - 1)
         group("w2", 0, 0, 0, 2, nc.scalar.copy, PICK + 2 * (2 * PACK - 1))
         quantise_x(1)
         group("w2", 1, 0, 0, 2, nc.vector.tensor_copy, XG)

import math
from contextlib import ExitStack

import concourse.mybir as mybir

K, H, T, S, M = 1024, 1024, 4096, 1024, 512
FLOPS = 2 * K * H * S + 2 * 2 * H * H * M

F32 = mybir.dt.float32
BF16 = mybir.dt.bfloat16
I32 = mybir.dt.int32
U32 = mybir.dt.uint32
U16 = mybir.dt.uint16
U8 = mybir.dt.uint8
FP8X4 = mybir.dt.float8_e4m3fn_x4
FP4X4 = mybir.dt.float4_e2m1fn_x4
ALU = mybir.AluOpType
ACT = mybir.ActivationFunctionType

P = 128
PACK = 4
PASS = P * PACK
BANK = 512
ROUNDER = 1.5 * 2.0**23
TURN = 2.0 * math.pi
KB = 1024


def tile_list_press_ghosting_features_kernel(
    tc, tab_words, tab_scales, offs, pos1, w1, gain, w2, w3_words, w3_scales, phase, skip, wgo, out
):
    nc = tc.nc
    with ExitStack() as ctx:
        keep = ctx.enter_context(tc.tile_pool(name="keep", bufs=1))
        laid = ctx.enter_context(tc.tile_pool(name="laid", bufs=1))
        ring = ctx.enter_context(tc.tile_pool(name="ring", bufs=2))
        psum = ctx.enter_context(tc.psum_pool(name="psum", bufs=8))

        def place(name, shape, dtype, kb):
            return laid.tile(shape, dtype, name=name, offset=kb * KB, align_bytes=64)

        TAB1, XG, PICK, TANH, PAGE, TAB0 = 10, 26, 32, 48, 80, 96

        warm = keep.tile([P, 1], F32, name="warm")
        warm_out = keep.tile([P, 1], F32, name="warm_out")
        nc.gpsimd.memset(warm[:], 0.0)
        nc.scalar.activation(warm_out[:], warm[:], ACT.Silu)
        offs_sb = keep.tile([P, S // 16], U16, name="offs_sb")
        pos_sb = keep.tile([P, M // 16], U16, name="pos_sb")
        nc.sync.dma_start(offs_sb[:], offs)
        w3_raw = keep.tile([P, 2, H // 2], I32, name="w3_raw", align_bytes=64)
        nc.sync.dma_start(w3_raw[:], w3_words.bitcast(I32).rearrange("a p c -> p a c"))

        tab_sc = place("tab_sc", [P, T // 4], I32, 0)
        w3_sc_raw = place("w3_sc_raw", [P, 2, H // 4], I32, 4)
        nc.vector.memset(tab_sc[:], 0)
        nc.vector.memset(w3_sc_raw[:], 0)
        gain_sb = keep.tile([P, 2, PACK], F32, name="gain_sb")
        skip_sb = keep.tile([P, 2, PACK], F32, name="skip_sb")
        phase_sb = keep.tile([P, 2, PACK], F32, name="phase_sb")
        skip_gain = keep.tile([P, 2, PACK], F32, name="skip_gain")
        phase_turns = keep.tile([P, 2, PACK], F32, name="phase_turns")

        tab = [place("tab0", [P, T], I32, TAB0), place("tab1", [P, T], I32, TAB1)]

        def load_tab(a):
            nc.sync.dma_start(tab[a][:], tab_words[a].rearrange("p t i -> p (t i)").bitcast(I32))

        raw = {}

        def load_w(name, w, a, b):
            t = ring.tile([P, PACK, PASS], F32, name="raw", tag="raw", bufs=6, align_bytes=64)
            nc.sync.dma_start(
                t[:], w[a * PASS : (a + 1) * PASS, b * PASS : (b + 1) * PASS].rearrange("(p j) c -> p j c", j=PACK)
            )
            raw[name, a, b] = t

        load_tab(0)
        for q in range(4):
            nc.sync.dma_start(tab_sc[32 * q : 32 * q + 8, :], tab_scales.bitcast(I32)[:, 4 * q : 4 * q + 4, :])
        for q in range(4):
            nc.sync.dma_start(
                w3_sc_raw[32 * q : 32 * q + 4, :, :],
                w3_scales.bitcast(I32)[:, 4 * q : 4 * q + 4, :].rearrange("a r c -> r a c"),
            )
        load_w("w1", w1, 0, 0)
        load_tab(1)
        load_w("w1", w1, 1, 0)
        nc.sync.dma_start(pos_sb[:], pos1)
        load_w("w1", w1, 0, 1)
        for dst, src in ((gain_sb, gain), (skip_sb, skip), (phase_sb, phase)):
            nc.sync.dma_start(dst[:], src.rearrange("(b p t) -> p b t", b=2, t=PACK))
        load_w("w1", w1, 1, 1)
        load_w("w2", w2, 0, 0)
        load_w("w2", w2, 1, 0)
        wgo_sb = keep.tile([P, PACK, M], F32, name="wgo_sb")
        for q in (0, 2, 1, 3):
            nc.sync.dma_start(wgo_sb[32 * q : 32 * q + 32], wgo.rearrange("(r t) m -> r t m", t=PACK))
        nc.gpsimd.tensor_tensor(skip_gain[:], skip_sb[:], gain_sb[:], ALU.mult)
        nc.gpsimd.tensor_scalar(phase_turns[:], phase_sb[:], 1.0 / TURN, 0.0, ALU.mult, ALU.add)

        w3_w = keep.tile([P, 2, H], U16, name="w3_w", align_bytes=64)
        w3_s = keep.tile([P, 2, H], U8, name="w3_s", align_bytes=64)
        nc.vector.tensor_copy(
            w3_w[:].rearrange("p a (b t m) -> p (a b) t m", b=2, t=PACK),
            w3_raw[:].bitcast(U16).rearrange("p a (b m t) -> p (a b) t m", b=2, t=PACK),
        )

        grouped, codes, scales = {}, {}, {}

        def group(name, a, b, t0, t1, copy, kb):
            g = place(f"g{name}_{a}{b}{t0}", [P, t1 - t0, P, PACK], BF16, kb)
            src = raw[name, a, b][:].rearrange("p j (m t) -> p m t j", t=PACK)[:, :, t0:t1, :]
            copy(g[:].rearrange("p t m j -> p m t j"), src)
            grouped[name, a, b, t0] = g

        def quantise(name, a, b, t0):
            g = grouped[name, a, b, t0]
            n = g.shape[1]
            c = keep.tile([P, n * P], U32, name=f"c{name}_{a}{b}{t0}", align_bytes=64)
            s = keep.tile([P, n * P], U8, name=f"s{name}_{a}{b}{t0}", align_bytes=64)
            nc.vector.quantize_mx(out=c[:].bitcast(FP8X4), scales=s[:], in_=g[:].rearrange("p t m j -> p (t m j)"))
            for t in range(n):
                codes[name, a, b, t0 + t] = c[:, t * P : (t + 1) * P]
                scales[name, a, b, t0 + t] = s[:, t * P : (t + 1) * P]

        v_w, v_s = {}, {}

        def gather_words(a, hf):
            nc.vector.tensor_copy(
                v_w[a][:, hf * BANK : (hf + 1) * BANK],
                tab[a][:].bitcast(U32).indirect(offs_sb[:, 32 * hf : 32 * hf + 32]),
            )

        def gather_scales(hf):
            t = keep.tile([P, BANK], U8, name=f"vs{hf}", align_bytes=64)
            nc.vector.tensor_copy(t[:], tab_sc[:].bitcast(U8).indirect(offs_sb[:, 32 * hf : 32 * hf + 32]))
            v_s[hf] = t

        banks = {}

        def mm1(b, t, hf, a):
            if a == 0:
                banks[b, t, hf] = psum.tile([P, BANK], F32, name="bank", tag="bank")
            nc.tensor.matmul_mx(
                out=banks[b, t, hf][:],
                lhsT=codes["w1", a, b, t].bitcast(FP8X4),
                lhsT_scale=scales["w1", a, b, t],
                rhs=v_w[a][:, hf * BANK : (hf + 1) * BANK].bitcast(FP8X4),
                rhs_scale=v_s[hf][4 * a : P, :],
                start=(a == 0),
                stop=(a == 1),
            )

        tanh_sb, picked, x_pairs = {}, {}, {}

        def read_out(b, t):
            th = place(f"tanh{b}{t}", [P, S], F32, TANH + 4 * (PACK * b + t))
            for hf in range(2):
                nc.scalar.activation(th[:, hf * BANK : (hf + 1) * BANK], banks[b, t, hf][:], ACT.Tanh)
            tanh_sb[b, t] = th

        def pick(b, t):
            g = place(f"picked{b}{t}", [P, M], F32, PICK + 2 * (PACK * b + t))
            nc.vector.tensor_copy(g[:], tanh_sb[b, t][:].indirect(pos_sb[:]))
            picked[b, t] = g

        def scale_round(b, t, on_vector):
            if t == 0:
                x_pairs[b] = place(f"x_pairs{b}", [P, 2, M, 2], BF16, PAGE + 4 * (1 - b))
            dst = x_pairs[b][:, t // 2, :, t % 2]
            if on_vector:
                nc.vector.tensor_scalar(dst, picked[b, t][:], gain_sb[:, b, t : t + 1], None, ALU.mult)
            else:
                nc.scalar.activation(dst, picked[b, t][:], ACT.Copy, scale=gain_sb[:, b, t : t + 1])

        def quantise_x(b):
            g = place(f"xg{b}", [P, M, 2], I32, XG)
            nc.vector.tensor_copy(g[:], x_pairs[b][:].rearrange("p u m e -> p u (m e)").bitcast(I32).rearrange("p u m -> p m u"))
            c = keep.tile([P, M], U32, name=f"xc{b}", align_bytes=64)
            s = keep.tile([P, M], U8, name=f"xs{b}", align_bytes=64)
            nc.vector.quantize_mx(
                out=c[:].bitcast(FP8X4), scales=s[:], in_=g[:].rearrange("p m u -> p (m u)").bitcast(BF16)
            )
            codes["x", b], scales["x", b] = c, s

        slices = [(b, t) for b in range(2) for t in range(PACK)]
        z_bank, lin, turns, frac = {}, {}, {}, {}

        def mm_z(i, a):
            b, t = slices[i]
            if a == 0:
                z_bank[i] = psum.tile([P, M], F32, name="z", tag="bank")
            c0 = b * PASS + t * P
            nc.tensor.matmul_mx(
                out=z_bank[i][:],
                lhsT=w3_w[:, a, c0 : c0 + P].bitcast(FP4X4),
                lhsT_scale=w3_s[:, a, c0 : c0 + P],
                rhs=codes["x", a][:].bitcast(FP8X4),
                rhs_scale=scales["x", a][:],
                start=(a == 0),
                stop=(a == 1),
            )

        v_w[0] = keep.tile([P, S], U32, name="v0", align_bytes=64)
        for hf in range(2):
            gather_scales(hf)
        for hf in range(2):
            gather_words(0, hf)
        group("w1", 0, 0, 0, PACK, nc.scalar.copy, 6)
        quantise("w1", 0, 0, 0)
        nc.vector.tensor_copy(
            w3_s[:].rearrange("p a (b t m) -> p (a b) t m", b=2, t=PACK),
            w3_sc_raw[:].bitcast(U8).rearrange("p a (b m t) -> p (a b) t m", b=2, t=PACK),
        )
        for t in range(PACK):
            for hf in range(2):
                mm1(0, t, hf, 0)
        v_w[1] = place("v1", [P, S], U32, 3)
        for hf in range(2):
            gather_words(1, hf)
        group("w1", 1, 0, 0, 2, nc.vector.tensor_copy, TAB1)
        group("w1", 1, 0, 2, PACK, nc.scalar.copy, XG)
        quantise("w1", 1, 0, 0)
        quantise("w1", 1, 0, 2)
        load_w("w2", w2, 0, 1)
        load_w("w2", w2, 1, 1)

        for t in range(PACK):
            for hf in range(2):
                mm1(0, t, hf, 1)
            read_out(0, t)
            if t in (0, 2):
                group("w1", t // 2, 1, 0, PACK, nc.vector.tensor_copy, TAB1)
                quantise("w1", t // 2, 1, 0)
            pick(0, t)
        for t in range(PACK):
            for hf in range(2):
                for a in range(2):
                    mm1(1, t, hf, a)
            read_out(1, t)
        for t in range(PACK):
            scale_round(0, t, False)
        for t in range(PACK):
            pick(1, t)
            if t == 1:
                quantise_x(0)
            scale_round(1, t, t >= 2)
        for i in range(2):
            mm_z(i, 0)
        group("w2", 0, 0, 0, 2, nc.scalar.copy, PICK + 2 * (2 * PACK - 1))
        quantise_x(1)
        group("w2", 1, 0, 0, 2, nc.vector.tensor_copy, XG)
        quantise("w2", 0, 0, 0)
        quantise("w2", 1, 0, 0)
        group("w2", 0, 0, 2, PACK, nc.vector.tensor_copy, XG + 2)
        quantise("w2", 0, 0, 2)

        page, y = {}, {}
        last = len(slices) - 1

        def to_turns(i):
            b, t = slices[i]
            if i >= 2:
                mm_z(i, 0)
            mm_z(i, 1)
            turns[i] = ring.tile([P, M], F32, name="turns", tag="turns", bufs=4)
            nc.scalar.activation(
                turns[i][:], z_bank[i][:], ACT.Identity, bias=phase_turns[:, b, t : t + 1], scale=1.0 / TURN
            )

        def take_fraction(i):
            whole = place(f"whole{i}", [P, M], U32, PAGE + 4 * i if i > 0 else PICK)
            nc.scalar.activation(whole[:], turns[i][:], ACT.Copy, bias=ROUNDER)
            frac[i] = ring.tile([P, M], F32, name="frac", tag="frac", bufs=3)
            nc.vector.scalar_tensor_tensor(
                frac[i][:], whole[:].bitcast(I32), ROUNDER, turns[i][:], ALU.subtract, ALU.subtract
            )

        def fill_page(i):
            b, t = slices[i]
            page[i] = place(f"page{i}", [P, S], F32, PAGE + 4 * i)
            nc.scalar.activation(page[i][:], tanh_sb[b, t][:], ACT.Copy, scale=skip_gain[:, b, t : t + 1])

        out_rows = out.rearrange("(b p t) j -> b t p j", b=2, t=PACK)

        def larger(i):
            b, t = slices[i]
            ln = psum.tile([P, M], F32, name="lin", tag="bank")
            for a in range(2):
                nc.tensor.matmul_mx(
                    out=ln[:],
                    lhsT=codes["w2", a, b, t].bitcast(FP8X4),
                    lhsT_scale=scales["w2", a, b, t],
                    rhs=codes["x", a][:].bitcast(FP8X4),
                    rhs_scale=scales["x", a][:],
                    start=(a == 0),
                    stop=(a == 1),
                )
            wave = ring.tile([P, M], F32, name="wave", tag="wave", bufs=3)
            nc.scalar.activation(wave[:], frac[i][:], ACT.Sin, scale=-TURN)
            y[i] = ring.tile([P, M], F32, name="y", tag="y", bufs=2)
            nc.vector.tensor_tensor(y[i][:], ln[:], wave[:], ALU.max)

        def put(i):
            b, t = slices[i]
            nc.vector.tensor_tensor(page[i][:].indirect(pos_sb[:]), y[i][:], wgo_sb[:, t, :], ALU.mult)
            nc.sync.dma_start(out_rows[b, t], page[i][:])

        later_groups = [(1, 0, 2), (0, 1, 0), (1, 1, 0), (0, 1, 2), (1, 1, 2)]
        fill_page(0)
        for i in range(2):
            to_turns(i)
            take_fraction(i)
        for i in range(len(slices)):
            if i + 2 <= last:
                to_turns(i + 2)
            larger(i)
            if i + 2 <= last:
                take_fraction(i + 2)
            if i > 0:
                fill_page(i)
            put(i)
            if i < len(later_groups):
                a, b, t0 = later_groups[i]
                group("w2", a, b, t0, t0 + 2, nc.scalar.copy, TANH + 4 * i)
                quantise("w2", a, b, t0)
